import numpy as np, ml_dtypes
CORES = [9,41,49,65,73,81,97,113,15,47,55,71,79,87,103,119]
N = 16
KB, QP, ROOT = 4, 128, 15
def setup_inputs(rng):
    return {"q": rng.standard_normal((N, 128, QP), dtype=np.float32).astype(ml_dtypes.bfloat16), "k": rng.standard_normal((N, 128, KB * 128), dtype=np.float32).astype(ml_dtypes.bfloat16), "v": rng.standard_normal((N, 128, KB * 128), dtype=np.float32).astype(ml_dtypes.bfloat16)}
def setup_inputs_big(rng):
    d = setup_inputs(rng)
    for k in ("q", "k", "v"): d[k] = (d[k].astype(np.float32) * 1024.0).astype(d[k].dtype)
    return d
def setup_inputs_small(rng):
    d = setup_inputs(rng)
    for k in ("q", "k", "v"): d[k] = (d[k].astype(np.float32) * (1 / 1024.0)).astype(d[k].dtype)
    return d
def setup_inputs_apart(rng):
    d = setup_inputs(rng)
    f = (10.0 ** rng.permutation(np.linspace(-1.5, 1.5, N))).astype(np.float32).reshape(N, 1, 1)
    for k in ("q", "k", "v"): d[k] = (d[k].astype(np.float32) * f).astype(d[k].dtype)
    return d
def reference(q, k, v):
    Q, K, V = q.astype(np.float64), k.astype(np.float64), v.astype(np.float64)
    o = np.zeros((128, QP))
    for j in range(N):
        for b in range(KB):
            o += V[j][:, 128 * b:128 * b + 128].T @ np.maximum(K[j][:, 128 * b:128 * b + 128].T @ Q[ROOT], 0.0)
    y = np.full((N, 128, QP), np.nan)
    y[ROOT] = o
    return {"y": y.astype(ml_dtypes.bfloat16 if q.dtype != np.float64 else np.float64)}

@@ -1,0 +1,269 @@
+from concourse.bass import DstId, RemoteDMATransfer
+from concourse.mybir import AluOpType
+
+P = 128
+H = P // 2
+KB = 4
+W = KB * P
+NB = 2 * KB
+NBANK = 7
+
+SPLIT_NEAR = True
+SPLIT_FAR = True
+USE_RELAY = True
+ROOT_NEAR = 3
+FAR_LAST = True
+NE_Q = 8
+NE_P = 8
+NE_ON = 16
+NE_KV = 8
+V_SKIP = 8
+
+SCRATCH = {
+    "q_sb": ("sbuf", [P, P], "bfloat16"),
+    "k_own": ("sbuf", [P, W], "bfloat16"),
+    "v_own": ("sbuf", [P, W], "bfloat16"),
+    "k_got": ("sbuf", [P, W], "bfloat16"),
+    "v_got": ("sbuf", [P, W], "bfloat16"),
+    "zero": ("sbuf", [P, P], "float32"),
+    "s_sb": ("sbuf", [P, NB * P], "bfloat16"),
+    "o_sb": ("sbuf", [P, P], "bfloat16"),
+    "land": ("sbuf", [P, 7 * P], "bfloat16"),
+    "o_ps": ("psum", [P, 512], "float32"),
+}
+for _b in range(NBANK):
+    SCRATCH["s_ps%d" % _b] = ("psum", [P, 512], "float32")
+
+SEMAPHORES = (["ld_q", "ld_k", "ld_v", "kf", "vf", "qa", "zs", "m2", "od", "ha", "sent", "st"]
+              + ["m1_%d" % b for b in range(NB)] + ["r_%d" % b for b in range(NB)]
+              + ["pa_%d" % i for i in range(12)] + ["ac_%d" % i for i in range(16)])
+
+
+def _plan(T, topo):
+    root = T.cores[T.root]
+    chips = {}
+    for c in T.cores:
+        chips.setdefault(topo.chip(c), []).append(c)
+    relay = [c for c in chips[topo.chip(root)] if c != root][0]
+    cols, kv_to, out_to = {root: (0, P)}, {relay: root}, {}
+    far_chips = [ch for ch in sorted(chips) if not all(topo.may_write(c, root) for c in chips[ch])]
+    near_chips = [ch for ch in sorted(chips) if ch not in far_chips and ch != topo.chip(root)]
+    calls = {root: [], relay: []}
+    first = ([relay] if USE_RELAY else [])
+    far_w = []
+    for ch in far_chips:
+        b = [c for c in chips[ch] if topo.may_write(c, root)][0]
+        a = [c for c in chips[ch] if c != b][0]
+        kv_to[a] = b
+        out_to[b] = root
+        far_w.append(b)
+        first.append(b)
+        if SPLIT_FAR:
+            kv_to[b] = a
+            cols[a], cols[b] = (0, H), (H, P)
+            out_to[a] = b
+            calls[b] = [(0, H, [a], NE_ON)]
+        else:
+            cols[b] = (0, P)
+    near_w = []
+    if SPLIT_NEAR:
+        mine, his = [], []
+        for ch in near_chips:
+            a = [c for c in chips[ch] if topo.die(c) == topo.die(relay)][0]
+            b = [c for c in chips[ch] if c != a][0]
+            kv_to[a], kv_to[b] = b, a
+            cols[a], cols[b] = (0, H), (H, P)
+            out_to[a] = out_to[b] = root
+            mine.append(b)
+            his.append(a)
+        calls[root].append((0, P, first, NE_Q))
+        if USE_RELAY:
+            if mine[:ROOT_NEAR]:
+                calls[root].append((H, P, mine[:ROOT_NEAR], NE_Q))
+            calls[relay].append((0, H, his, NE_Q))
+            if mine[ROOT_NEAR:]:
+                calls[relay].append((H, P, mine[ROOT_NEAR:], NE_Q))
+        else:
+            calls[root].append((H, P, mine, NE_Q))
+            calls[root].append((0, H, his, NE_Q))
+        for x, y in zip(mine, his):
+            near_w += [x, y]
+    else:
+        for i, ch in enumerate(near_chips):
+            by_root = (not USE_RELAY) or i < ROOT_NEAR
+            d = topo.die(root if by_root else relay)
+            w = [c for c in chips[ch] if topo.die(c) == d][0]
+            a = [c for c in chips[ch] if c != w][0]
+            kv_to[a] = w
+            cols[w] = (0, P)
+            out_to[w] = root
+            near_w.append(w)
+            if by_root:
+                first.append(w)
+        calls[root].append((0, P, first, NE_Q))
+        rest = [w for w in near_w if w not in first]
+        if rest:
+            calls[relay].append((0, P, rest, NE_Q))
+    senders = (near_w + far_w) if FAR_LAST else (far_w + near_w)
+    pieces, off = [], 0
+    for s in senders:
+        c0, c1 = (0, P) if (SPLIT_FAR and s in far_w) else cols[s]
+        pieces.append((s, off, c0, c1))
+        off += c1 - c0
+    qn = {}
+    for cl in calls.values():
+        for _, _, dsts, n in cl:
+            for d in dsts:
+                qn[d] = n
+    return dict(root=root, relay=relay, cols=cols, kv_to=kv_to, out_to=out_to, calls=calls, pieces=pieces, qn=qn)
+
+
+def _engines(topo, src, dsts, n, skip=0):
+    m = topo.mask(src, dsts[0])
+    for d in dsts[1:]:
+        m &= topo.mask(src, d)
+    out, k = 0, 0
+    for b in range(m.bit_length()):
+        if (m >> b) & 1:
+            if skip <= k < skip + n:
+                out |= 1 << b
+            k += 1
+    return out
+
+
+def _write(g, topo, src, dst, out_ap, in_ap, remote_sem, local_sem, n, skip=0):
+    rid, pid, _ = topo.addr(dst)
+    g.remote_dma(out_ap=out_ap, in_ap=in_ap, remote_sem=remote_sem, local_sem=local_sem, pid=pid, routing_id=rid,
+                 dma_engine_mask=_engines(topo, src, [dst], n, skip))
+
+
+def rank_program(g, core, T, topo):
+    if T.rank_of(core) is None:
+        return
+    S = T.sem
+    pl = _plan(T, topo)
+    root = pl["root"]
+    works = core in pl["cols"]
+    kv_to = pl["kv_to"].get(core)
+    calls = pl["calls"].get(core, [])
+    te, ve = g.tensor, g.vector
+    sent = 0
+
+    if works:
+        ve.memset(T.zero[:, :], 0.0).then_inc(S.zs, 1)
+    if core == root:
+        g.sync.dma_start(T.q_sb[:, :], T.q[:, :]).then_inc(S.ld_q, 16)
+        g.sync.dma_start(T.k_own[:, :], T.k[:, :]).then_inc(S.ld_k, 16)
+        g.sync.dma_start(T.v_own[:, :], T.v[:, :]).then_inc(S.ld_v, 16)
+    else:
+        g.sync.dma_start(T.k_own[:, :], T.k[:, :]).then_inc(S.ld_k, 16)
+        g.scalar.dma_start(T.v_own[:, :], T.v[:, :]).then_inc(S.ld_v, 16)
+
+    def spread():
+        n = 0
+        if not calls:
+            return n
+        if core == root:
+            g.wait_ge(S.ld_q, 16)
+        else:
+            g.wait_ge(S.qa, pl["qn"][core])
+        for c0, c1, dsts, ne in calls:
+            ids = []
+            for w in dsts:
+                rid, pid, _ = topo.addr(w)
+                ids.append(DstId(rid=rid, pnc=pid))
+            g.remote_dma_fused([RemoteDMATransfer(dst_ids=ids, dma_engine_mask=_engines(topo, core, dsts, ne),
+                                                  remote_sem=S.qa, srcs=[T.q_sb[:, c0:c1]],
+                                                  dsts=[T.q_sb[:, c0:c1] for _ in dsts], alu_op=0)], local_sem=S.sent)
+            n += ne
+        return n
+
+    if kv_to is not None:
+        g.wait_ge(S.ld_k, 16)
+        _write(g, topo, core, kv_to, T.k_got[:, :], T.k_own[:, :], S.kf, S.sent, NE_KV)
+        if not works:
+            sent += spread()
+        g.wait_ge(S.ld_v, 16)
+        _write(g, topo, core, kv_to, T.v_got[:, :], T.v_own[:, :], S.vf, S.sent, NE_KV, V_SKIP)
+        sent += 2 * NE_KV
+        if works:
+            sent += spread()
+    else:
+        sent += spread()
+    if not works:
+        g.wait_ge(S.sent, sent)
+        return
+
+    c0, c1 = pl["cols"][core]
+    wd = c1 - c0
+    if core == root:
+        te.wait_ge(S.ld_q, 16)
+    else:
+        te.wait_ge(S.qa, pl["qn"][core])
+    te.wait_ge(S.ld_k, 16)
+    for b in range(NB):
+        if b == KB:
+            te.wait_ge(S.kf, NE_KV)
+        if b >= NBANK:
+            te.wait_ge(S["r_%d" % (b - NBANK)], 1)
+        kk = T.k_own if b < KB else T.k_got
+        x = (b % KB) * P
+        te.matmul(T["s_ps%d" % (b % NBANK)][:, 0:wd], kk[:, x:x + P], T.q_sb[:, c0:c1], True, True).then_inc(
+            S["m1_%d" % b], 1)
+    ve.wait_ge(S.zs, 1)
+    for b in range(NB):
+        ve.wait_ge(S["m1_%d" % b], 1)
+        ve.tensor_tensor(T.s_sb[:, b * P:b * P + wd], T["s_ps%d" % (b % NBANK)][:, 0:wd], T.zero[:, 0:wd],
+                         AluOpType.max).then_inc(S["r_%d" % b], 1)
+    te.wait_ge(S.ld_v, 16)
+    for b in range(NB):
+        if b == KB:
+            te.wait_ge(S.vf, NE_KV)
+        te.wait_ge(S["r_%d" % b], 1)
+        vv = T.v_own if b < KB else T.v_got
+        x = (b % KB) * P
+        mm = te.matmul(T.o_ps[:, 0:wd], vv[:, x:x + P], T.s_sb[:, b * P:b * P + wd], b == 0, b == NB - 1)
+        if b == NB - 1:
+            mm.then_inc(S.m2, 1)
+    ve.wait_ge(S.m2, 1)
+
+    if core != root:
+        ve.tensor_copy(T.o_sb[:, c0:c1], T.o_ps[:, 0:wd]).then_inc(S.od, 1)
+        g.wait_ge(S.od, 1)
+        to = pl["out_to"][core]
+        if to != root:
+            _write(g, topo, core, to, T.o_sb[:, c0:c1], T.o_sb[:, c0:c1], S.ha, S.sent, NE_ON)
+            sent += NE_ON
+        else:
+            i = [j for j, p in enumerate(pl["pieces"]) if p[0] == core][0]
+            _, off, a0, a1 = pl["pieces"][i]
+            if a1 - a0 != wd:
+                g.wait_ge(S.ha, NE_ON)
+            _write(g, topo, core, root, T.land[:, off:off + a1 - a0], T.o_sb[:, a0:a1], S["pa_%d" % i], S.sent, NE_P)
+            sent += NE_P
+        g.wait_ge(S.sent, sent)
+        return
+
+    ops = []
+    for i, (s, off, a0, a1) in enumerate(pl["pieces"]):
+        for h0 in range(a0, a1, H):
+            ops.append((i, off + h0 - a0, h0 // H))
+    left = [sum(1 for o in ops if o[2] == h) for h in (0, 1)]
+    turn, prev, seen = [0, 0], [None, None], set()
+    for j, (i, off, h) in enumerate(ops):
+        if i not in seen:
+            ve.wait_ge(S["pa_%d" % i], NE_P)
+            seen.add(i)
+        if prev[h] is not None:
+            ve.wait_ge(S["ac_%d" % prev[h]], 1)
+        left[h] -= 1
+        src = T.o_ps[:, turn[h] * P + h * H:turn[h] * P + h * H + H]
+        turn[h] ^= 1
+        dst = T.o_sb[:, h * H:h * H + H] if left[h] == 0 else T.o_ps[:, turn[h] * P + h * H:turn[h] * P + h * H + H]
+        ve.tensor_tensor(dst, src, T.land[:, off:off + H], AluOpType.add).then_inc(S["ac_%d" % j], 1)
+        prev[h] = j
+    for h in (0, 1):
+        g.sync.wait_ge(S["ac_%d" % prev[h]], 1)
+    g.sync.dma_start(T.y[:, :], T.o_sb[:, :]).then_inc(S.st, 16)
+    g.sync.wait_ge(S.st, 16)
+    g.wait_ge(S.sent, sent)

@@ -8,16 +8,16 @@ W = KB * P
 NB = 2 * KB
 NBANK = 7
 
-SPLIT_NEAR = True
-SPLIT_FAR = True
-USE_RELAY = True
-ROOT_NEAR = 3
-FAR_LAST = True
+FAR = "sss"
+XN = 96
+ROOT_SEQ = [("f", ["R", "A0", "A1", "A2"]), ("n1", ["b0", "b1", "b2"])]
+RELAY_SEQ = [("n0", ["a0", "a1", "a2", "a3"]), ("n1", ["b3"])]
+ORDER = ["a0", "b0", "a1", "b1", "B0", "a2", "b2", "B1", "a3", "b3", "B2"]
 NE_Q = 8
 NE_P = 8
 NE_ON = 16
-NE_KV = 8
-V_SKIP = 8
+KV_ALL = (16, 16, 0)
+KV_RELAY = (8, 8, 8)
 
 SCRATCH = {
     "q_sb": ("sbuf", [P, P], "bfloat16"),
@@ -30,13 +30,17 @@ SCRATCH = {
     "o_sb": ("sbuf", [P, P], "bfloat16"),
     "land": ("sbuf", [P, 7 * P], "bfloat16"),
     "o_ps": ("psum", [P, 512], "float32"),
+    "id_src": ("sbuf", [P, P + 1], "bfloat16"),
+    "id_dr": ("dram", [P * (P + 1)], "bfloat16"),
+    "ident": ("sbuf", [P, P], "bfloat16"),
 }
 for _b in range(NBANK):
     SCRATCH["s_ps%d" % _b] = ("psum", [P, 512], "float32")
 
-SEMAPHORES = (["ld_q", "ld_k", "ld_v", "kf", "vf", "qa", "zs", "m2", "od", "ha", "sent", "st"]
+SEMAPHORES = (["ld_q", "ld_k0", "ld_k", "ld_v", "kf0", "kf", "vf", "qa", "zs", "m2", "od", "ha", "sent", "st",
+               "i0", "i1", "i2", "i3"]
               + ["m1_%d" % b for b in range(NB)] + ["r_%d" % b for b in range(NB)]
-              + ["pa_%d" % i for i in range(12)] + ["ac_%d" % i for i in range(16)])
+              + ["pa_%d" % i for i in range(12)])
 
 
 def _plan(T, topo):
@@ -45,69 +49,41 @@ def _plan(T, topo):
     for c in T.cores:
         chips.setdefault(topo.chip(c), []).append(c)
     relay = [c for c in chips[topo.chip(root)] if c != root][0]
-    cols, kv_to, out_to = {root: (0, P)}, {relay: root}, {}
     far_chips = [ch for ch in sorted(chips) if not all(topo.may_write(c, root) for c in chips[ch])]
     near_chips = [ch for ch in sorted(chips) if ch not in far_chips and ch != topo.chip(root)]
-    calls = {root: [], relay: []}
-    first = ([relay] if USE_RELAY else [])
-    far_w = []
-    for ch in far_chips:
+    name, sib = {"R": relay}, {}
+    cols, kv_to, out_to = {root: (0, P)}, {relay: root}, {}
+    for i, ch in enumerate(far_chips):
         b = [c for c in chips[ch] if topo.may_write(c, root)][0]
         a = [c for c in chips[ch] if c != b][0]
-        kv_to[a] = b
-        out_to[b] = root
-        far_w.append(b)
-        first.append(b)
-        if SPLIT_FAR:
-            kv_to[b] = a
-            cols[a], cols[b] = (0, H), (H, P)
-            out_to[a] = b
-            calls[b] = [(0, H, [a], NE_ON)]
-        else:
+        name["A%d" % i], name["B%d" % i] = a, b
+        sib[a], sib[b] = b, a
+        kv_to[a], out_to[b] = b, root
+        if FAR[i] == "u":
             cols[b] = (0, P)
-    near_w = []
-    if SPLIT_NEAR:
-        mine, his = [], []
-        for ch in near_chips:
-            a = [c for c in chips[ch] if topo.die(c) == topo.die(relay)][0]
-            b = [c for c in chips[ch] if c != a][0]
-            kv_to[a], kv_to[b] = b, a
-            cols[a], cols[b] = (0, H), (H, P)
-            out_to[a] = out_to[b] = root
-            mine.append(b)
-            his.append(a)
-        calls[root].append((0, P, first, NE_Q))
-        if USE_RELAY:
-            if mine[:ROOT_NEAR]:
-                calls[root].append((H, P, mine[:ROOT_NEAR], NE_Q))
-            calls[relay].append((0, H, his, NE_Q))
-            if mine[ROOT_NEAR:]:
-                calls[relay].append((H, P, mine[ROOT_NEAR:], NE_Q))
         else:
-            calls[root].append((H, P, mine, NE_Q))
-            calls[root].append((0, H, his, NE_Q))
-        for x, y in zip(mine, his):
-            near_w += [x, y]
-    else:
-        for i, ch in enumerate(near_chips):
-            by_root = (not USE_RELAY) or i < ROOT_NEAR
-            d = topo.die(root if by_root else relay)
-            w = [c for c in chips[ch] if topo.die(c) == d][0]
-            a = [c for c in chips[ch] if c != w][0]
-            kv_to[a] = w
-            cols[w] = (0, P)
-            out_to[w] = root
-            near_w.append(w)
-            if by_root:
-                first.append(w)
-        calls[root].append((0, P, first, NE_Q))
-        rest = [w for w in near_w if w not in first]
-        if rest:
-            calls[relay].append((0, P, rest, NE_Q))
-    senders = (near_w + far_w) if FAR_LAST else (far_w + near_w)
+            kv_to[b], out_to[a] = a, b
+            cols[a], cols[b] = (0, H), (H, P)
+    for i, ch in enumerate(near_chips):
+        a = [c for c in chips[ch] if topo.die(c) == topo.die(relay)][0]
+        b = [c for c in chips[ch] if c != a][0]
+        name["a%d" % i], name["b%d" % i] = a, b
+        sib[a], sib[b] = b, a
+        kv_to[a], kv_to[b] = b, a
+        cols[a], cols[b] = (0, XN), (XN, P)
+        out_to[a] = out_to[b] = root
+    rng = {"f": (0, P), "h0": (0, H), "h1": (H, P), "n0": (0, XN), "n1": (XN, P)}
+    calls = {}
+    for src, seq in ((root, ROOT_SEQ), (relay, RELAY_SEQ)):
+        calls[src] = [(rng[kind][0], rng[kind][1], [name[x] for x in lst], NE_Q) for kind, lst in seq]
+    served = set(d for cl in calls.values() for _, _, dsts, _ in cl for d in dsts)
+    for c in sorted(cols):
+        if c != root and c not in served:
+            calls.setdefault(sib[c], []).append((cols[c][0], cols[c][1], [c], NE_ON))
     pieces, off = [], 0
-    for s in senders:
-        c0, c1 = (0, P) if (SPLIT_FAR and s in far_w) else cols[s]
+    for x in ORDER:
+        s = name[x]
+        c0, c1 = (0, P) if x[0] == "B" else cols[s]
         pieces.append((s, off, c0, c1))
         off += c1 - c0
     qn = {}
@@ -142,7 +118,7 @@ def rank_program(g, core, T, topo):
         return
     S = T.sem
     pl = _plan(T, topo)
-    root = pl["root"]
+    root, relay = pl["root"], pl["relay"]
     works = core in pl["cols"]
     kv_to = pl["kv_to"].get(core)
     calls = pl["calls"].get(core, [])
@@ -153,11 +129,16 @@ def rank_program(g, core, T, topo):
         ve.memset(T.zero[:, :], 0.0).then_inc(S.zs, 1)
     if core == root:
         g.sync.dma_start(T.q_sb[:, :], T.q[:, :]).then_inc(S.ld_q, 16)
-        g.sync.dma_start(T.k_own[:, :], T.k[:, :]).then_inc(S.ld_k, 16)
-        g.sync.dma_start(T.v_own[:, :], T.v[:, :]).then_inc(S.ld_v, 16)
-    else:
-        g.sync.dma_start(T.k_own[:, :], T.k[:, :]).then_inc(S.ld_k, 16)
-        g.scalar.dma_start(T.v_own[:, :], T.v[:, :]).then_inc(S.ld_v, 16)
+        ve.memset(T.id_src[:, :], 0.0).then_inc(S.i0, 1)
+        ve.wait_ge(S.i0, 1)
+        ve.memset(T.id_src[:, 0:1], 1.0).then_inc(S.i1, 1)
+        g.scalar.wait_ge(S.i1, 1)
+        g.scalar.dma_start(T.id_dr[0:P * (P + 1)], T.id_src[:, :]).then_inc(S.i2, 16)
+        g.scalar.wait_ge(S.i2, 16)
+        g.scalar.dma_start(T.ident[:, :], T.id_dr[0:P * P]).then_inc(S.i3, 16)
+    g.sync.dma_start(T.k_own[:, 0:P], T.k[:, 0:P]).then_inc(S.ld_k0, 16)
+    g.sync.dma_start(T.k_own[:, P:W], T.k[:, P:W]).then_inc(S.ld_k, 16)
+    g.sync.dma_start(T.v_own[:, :], T.v[:, :]).then_inc(S.ld_v, 16)
 
     def spread():
         n = 0
@@ -179,13 +160,16 @@ def rank_program(g, core, T, topo):
         return n
 
     if kv_to is not None:
+        n0, nr, sk = KV_RELAY if core == relay else KV_ALL
+        g.wait_ge(S.ld_k0, 16)
+        _write(g, topo, core, kv_to, T.k_got[:, 0:P], T.k_own[:, 0:P], S.kf0, S.sent, n0)
         g.wait_ge(S.ld_k, 16)
-        _write(g, topo, core, kv_to, T.k_got[:, :], T.k_own[:, :], S.kf, S.sent, NE_KV)
+        _write(g, topo, core, kv_to, T.k_got[:, P:W], T.k_own[:, P:W], S.kf, S.sent, nr, sk)
         if not works:
             sent += spread()
         g.wait_ge(S.ld_v, 16)
-        _write(g, topo, core, kv_to, T.v_got[:, :], T.v_own[:, :], S.vf, S.sent, NE_KV, V_SKIP)
-        sent += 2 * NE_KV
+        _write(g, topo, core, kv_to, T.v_got[:, :], T.v_own[:, :], S.vf, S.sent, nr, sk)
+        sent += n0 + 2 * nr
         if works:
             sent += spread()
     else:
@@ -196,14 +180,18 @@ def rank_program(g, core, T, topo):
 
     c0, c1 = pl["cols"][core]
     wd = c1 - c0
+    n0, nr, _ = KV_RELAY if core == root else KV_ALL
     if core == root:
         te.wait_ge(S.ld_q, 16)
     else:
         te.wait_ge(S.qa, pl["qn"][core])
+    te.wait_ge(S.ld_k0, 16)
     te.wait_ge(S.ld_k, 16)
     for b in range(NB):
         if b == KB:
-            te.wait_ge(S.kf, NE_KV)
+            te.wait_ge(S.kf0, n0)
+        if b == KB + 1:
+            te.wait_ge(S.kf, nr)
         if b >= NBANK:
             te.wait_ge(S["r_%d" % (b - NBANK)], 1)
         kk = T.k_own if b < KB else T.k_got
@@ -218,13 +206,19 @@ def rank_program(g, core, T, topo):
     te.wait_ge(S.ld_v, 16)
     for b in range(NB):
         if b == KB:
-            te.wait_ge(S.vf, NE_KV)
+            te.wait_ge(S.vf, nr)
         te.wait_ge(S["r_%d" % b], 1)
         vv = T.v_own if b < KB else T.v_got
         x = (b % KB) * P
-        mm = te.matmul(T.o_ps[:, 0:wd], vv[:, x:x + P], T.s_sb[:, b * P:b * P + wd], b == 0, b == NB - 1)
-        if b == NB - 1:
-            mm.then_inc(S.m2, 1)
+        mm = te.matmul(T.o_ps[:, 0:wd], vv[:, x:x + P], T.s_sb[:, b * P:b * P + wd], b == 0,
+                       b == NB - 1 and core != root)
+    if core == root:
+        te.wait_ge(S.i3, 16)
+        for i, (s, off, a0, a1) in enumerate(pl["pieces"]):
+            te.wait_ge(S["pa_%d" % i], NE_P)
+            mm = te.matmul(T.o_ps[:, a0:a1], T.ident[:, :], T.land[:, off:off + a1 - a0], False,
+                           i == len(pl["pieces"]) - 1)
+    mm.then_inc(S.m2, 1)
     ve.wait_ge(S.m2, 1)
 
     if core != root:
@@ -244,26 +238,8 @@ def rank_program(g, core, T, topo):
         g.wait_ge(S.sent, sent)
         return
 
-    ops = []
-    for i, (s, off, a0, a1) in enumerate(pl["pieces"]):
-        for h0 in range(a0, a1, H):
-            ops.append((i, off + h0 - a0, h0 // H))
-    left = [sum(1 for o in ops if o[2] == h) for h in (0, 1)]
-    turn, prev, seen = [0, 0], [None, None], set()
-    for j, (i, off, h) in enumerate(ops):
-        if i not in seen:
-            ve.wait_ge(S["pa_%d" % i], NE_P)
-            seen.add(i)
-        if prev[h] is not None:
-            ve.wait_ge(S["ac_%d" % prev[h]], 1)
-        left[h] -= 1
-        src = T.o_ps[:, turn[h] * P + h * H:turn[h] * P + h * H + H]
-        turn[h] ^= 1
-        dst = T.o_sb[:, h * H:h * H + H] if left[h] == 0 else T.o_ps[:, turn[h] * P + h * H:turn[h] * P + h * H + H]
-        ve.tensor_tensor(dst, src, T.land[:, off:off + H], AluOpType.add).then_inc(S["ac_%d" % j], 1)
-        prev[h] = j
-    for h in (0, 1):
-        g.sync.wait_ge(S["ac_%d" % prev[h]], 1)
+    ve.tensor_copy(T.o_sb[:, :], T.o_ps[:, 0:P]).then_inc(S.od, 1)
+    g.sync.wait_ge(S.od, 1)
     g.sync.dma_start(T.y[:, :], T.o_sb[:, :]).then_inc(S.st, 16)
     g.sync.wait_ge(S.st, 16)
     g.wait_ge(S.sent, sent)

from concourse.bass import DstId, RemoteDMATransfer
from concourse.mybir import AluOpType

P = 128
H = P // 2
KB = 4
W = KB * P
NB = 2 * KB
NBANK = 7

FAR = "sss"
XN = 96
ROOT_SEQ = [("f", ["R", "A0", "A1", "A2"]), ("n1", ["b0", "b1", "b2"])]
RELAY_SEQ = [("n0", ["a0", "a1", "a2", "a3"]), ("n1", ["b3"])]
ORDER = ["a0", "b0", "a1", "b1", "B0", "a2", "b2", "B1", "a3", "b3", "B2"]
NE_Q = 8
NE_P = 8
NE_ON = 16
KV_ALL = (16, 16, 0)
KV_RELAY = (8, 8, 8)

SCRATCH = {
    "q_sb": ("sbuf", [P, P], "bfloat16"),
    "k_own": ("sbuf", [P, W], "bfloat16"),
    "v_own": ("sbuf", [P, W], "bfloat16"),
    "k_got": ("sbuf", [P, W], "bfloat16"),
    "v_got": ("sbuf", [P, W], "bfloat16"),
    "zero": ("sbuf", [P, P], "float32"),
    "s_sb": ("sbuf", [P, NB * P], "bfloat16"),
    "o_sb": ("sbuf", [P, P], "bfloat16"),
    "land": ("sbuf", [P, 7 * P], "bfloat16"),
    "o_ps": ("psum", [P, 512], "float32"),
    "id_src": ("sbuf", [P, P + 1], "bfloat16"),
    "id_dr": ("dram", [P * (P + 1)], "bfloat16"),
    "ident": ("sbuf", [P, P], "bfloat16"),
}
for _b in range(NBANK):
    SCRATCH["s_ps%d" % _b] = ("psum", [P, 512], "float32")

SEMAPHORES = (["ld_q", "ld_k0", "ld_k", "ld_v", "kf0", "kf", "vf", "qa", "zs", "m2", "od", "ha", "sent", "st",
               "i0", "i1", "i2", "i3"]
              + ["m1_%d" % b for b in range(NB)] + ["r_%d" % b for b in range(NB)]
              + ["pa_%d" % i for i in range(12)])


def _plan(T, topo):
    root = T.cores[T.root]
    chips = {}
    for c in T.cores:
        chips.setdefault(topo.chip(c), []).append(c)
    relay = [c for c in chips[topo.chip(root)] if c != root][0]
    far_chips = [ch for ch in sorted(chips) if not all(topo.may_write(c, root) for c in chips[ch])]
    near_chips = [ch for ch in sorted(chips) if ch not in far_chips and ch != topo.chip(root)]
    name, sib = {"R": relay}, {}
    cols, kv_to, out_to = {root: (0, P)}, {relay: root}, {}
    for i, ch in enumerate(far_chips):
        b = [c for c in chips[ch] if topo.may_write(c, root)][0]
        a = [c for c in chips[ch] if c != b][0]
        name["A%d" % i], name["B%d" % i] = a, b
        sib[a], sib[b] = b, a
        kv_to[a], out_to[b] = b, root
        if FAR[i] == "u":
            cols[b] = (0, P)
        else:
            kv_to[b], out_to[a] = a, b
            cols[a], cols[b] = (0, H), (H, P)
    for i, ch in enumerate(near_chips):
        a = [c for c in chips[ch] if topo.die(c) == topo.die(relay)][0]
        b = [c for c in chips[ch] if c != a][0]
        name["a%d" % i], name["b%d" % i] = a, b
        sib[a], sib[b] = b, a
        kv_to[a], kv_to[b] = b, a
        cols[a], cols[b] = (0, XN), (XN, P)
        out_to[a] = out_to[b] = root
    rng = {"f": (0, P), "h0": (0, H), "h1": (H, P), "n0": (0, XN), "n1": (XN, P)}
    calls = {}
    for src, seq in ((root, ROOT_SEQ), (relay, RELAY_SEQ)):
        calls[src] = [(rng[kind][0], rng[kind][1], [name[x] for x in lst], NE_Q) for kind, lst in seq]
    served = set(d for cl in calls.values() for _, _, dsts, _ in cl for d in dsts)
    for c in sorted(cols):
        if c != root and c not in served:
            calls.setdefault(sib[c], []).append((cols[c][0], cols[c][1], [c], NE_ON))
    pieces, off = [], 0
    for x in ORDER:
        s = name[x]
        c0, c1 = (0, P) if x[0] == "B" else cols[s]
        pieces.append((s, off, c0, c1))
        off += c1 - c0
    qn = {}
    for cl in calls.values():
        for _, _, dsts, n in cl:
            for d in dsts:
                qn[d] = n
    return dict(root=root, relay=relay, cols=cols, kv_to=kv_to, out_to=out_to, calls=calls, pieces=pieces, qn=qn)


def _engines(topo, src, dsts, n, skip=0):
    m = topo.mask(src, dsts[0])
    for d in dsts[1:]:
        m &= topo.mask(src, d)
    out, k = 0, 0
    for b in range(m.bit_length()):
        if (m >> b) & 1:
            if skip <= k < skip + n:
                out |= 1 << b
            k += 1
    return out


def _write(g, topo, src, dst, out_ap, in_ap, remote_sem, local_sem, n, skip=0):
    rid, pid, _ = topo.addr(dst)
    g.remote_dma(out_ap=out_ap, in_ap=in_ap, remote_sem=remote_sem, local_sem=local_sem, pid=pid, routing_id=rid,
                 dma_engine_mask=_engines(topo, src, [dst], n, skip))


def rank_program(g, core, T, topo):
    if T.rank_of(core) is None:
        return
    S = T.sem
    pl = _plan(T, topo)
    root, relay = pl["root"], pl["relay"]
    works = core in pl["cols"]
    kv_to = pl["kv_to"].get(core)
    calls = pl["calls"].get(core, [])
    te, ve = g.tensor, g.vector
    sent = 0

    if works:
        ve.memset(T.zero[:, :], 0.0).then_inc(S.zs, 1)
    if core == root:
        g.sync.dma_start(T.q_sb[:, :], T.q[:, :]).then_inc(S.ld_q, 16)
        ve.memset(T.id_src[:, :], 0.0).then_inc(S.i0, 1)
        ve.wait_ge(S.i0, 1)
        ve.memset(T.id_src[:, 0:1], 1.0).then_inc(S.i1, 1)
        g.scalar.wait_ge(S.i1, 1)
        g.scalar.dma_start(T.id_dr[0:P * (P + 1)], T.id_src[:, :]).then_inc(S.i2, 16)
        g.scalar.wait_ge(S.i2, 16)
        g.scalar.dma_start(T.ident[:, :], T.id_dr[0:P * P]).then_inc(S.i3, 16)
    g.sync.dma_start(T.k_own[:, 0:P], T.k[:, 0:P]).then_inc(S.ld_k0, 16)
    g.sync.dma_start(T.k_own[:, P:W], T.k[:, P:W]).then_inc(S.ld_k, 16)
    g.sync.dma_start(T.v_own[:, :], T.v[:, :]).then_inc(S.ld_v, 16)

    def spread():
        n = 0
        if not calls:
            return n
        if core == root:
            g.wait_ge(S.ld_q, 16)
        else:
            g.wait_ge(S.qa, pl["qn"][core])
        for c0, c1, dsts, ne in calls:
            ids = []
            for w in dsts:
                rid, pid, _ = topo.addr(w)
                ids.append(DstId(rid=rid, pnc=pid))
            g.remote_dma_fused([RemoteDMATransfer(dst_ids=ids, dma_engine_mask=_engines(topo, core, dsts, ne),
                                                  remote_sem=S.qa, srcs=[T.q_sb[:, c0:c1]],
                                                  dsts=[T.q_sb[:, c0:c1] for _ in dsts], alu_op=0)], local_sem=S.sent)
            n += ne
        return n

    if kv_to is not None:
        n0, nr, sk = KV_RELAY if core == relay else KV_ALL
        g.wait_ge(S.ld_k0, 16)
        _write(g, topo, core, kv_to, T.k_got[:, 0:P], T.k_own[:, 0:P], S.kf0, S.sent, n0)
        g.wait_ge(S.ld_k, 16)
        _write(g, topo, core, kv_to, T.k_got[:, P:W], T.k_own[:, P:W], S.kf, S.sent, nr, sk)
        if not works:
            sent += spread()
        g.wait_ge(S.ld_v, 16)
        _write(g, topo, core, kv_to, T.v_got[:, :], T.v_own[:, :], S.vf, S.sent, nr, sk)
        sent += n0 + 2 * nr
        if works:
            sent += spread()
    else:
        sent += spread()
    if not works:
        g.wait_ge(S.sent, sent)
        return

    c0, c1 = pl["cols"][core]
    wd = c1 - c0
    n0, nr, _ = KV_RELAY if core == root else KV_ALL
    if core == root:
        te.wait_ge(S.ld_q, 16)
    else:
        te.wait_ge(S.qa, pl["qn"][core])
    te.wait_ge(S.ld_k0, 16)
    te.wait_ge(S.ld_k, 16)
    for b in range(NB):
        if b == KB:
            te.wait_ge(S.kf0, n0)
        if b == KB + 1:
            te.wait_ge(S.kf, nr)
        if b >= NBANK:
            te.wait_ge(S["r_%d" % (b - NBANK)], 1)
        kk = T.k_own if b < KB else T.k_got
        x = (b % KB) * P
        te.matmul(T["s_ps%d" % (b % NBANK)][:, 0:wd], kk[:, x:x + P], T.q_sb[:, c0:c1], True, True).then_inc(
            S["m1_%d" % b], 1)
    ve.wait_ge(S.zs, 1)
    for b in range(NB):
        ve.wait_ge(S["m1_%d" % b], 1)
        ve.tensor_tensor(T.s_sb[:, b * P:b * P + wd], T["s_ps%d" % (b % NBANK)][:, 0:wd], T.zero[:, 0:wd],
                         AluOpType.max).then_inc(S["r_%d" % b], 1)
    te.wait_ge(S.ld_v, 16)
    for b in range(NB):
        if b == KB:
            te.wait_ge(S.vf, nr)
        te.wait_ge(S["r_%d" % b], 1)
        vv = T.v_own if b < KB else T.v_got
        x = (b % KB) * P
        mm = te.matmul(T.o_ps[:, 0:wd], vv[:, x:x + P], T.s_sb[:, b * P:b * P + wd], b == 0,
                       b == NB - 1 and core != root)
    if core == root:
        te.wait_ge(S.i3, 16)
        for i, (s, off, a0, a1) in enumerate(pl["pieces"]):
            te.wait_ge(S["pa_%d" % i], NE_P)
            mm = te.matmul(T.o_ps[:, a0:a1], T.ident[:, :], T.land[:, off:off + a1 - a0], False,
                           i == len(pl["pieces"]) - 1)
    mm.then_inc(S.m2, 1)
    ve.wait_ge(S.m2, 1)

    if core != root:
        ve.tensor_copy(T.o_sb[:, c0:c1], T.o_ps[:, 0:wd]).then_inc(S.od, 1)
        g.wait_ge(S.od, 1)
        to = pl["out_to"][core]
        if to != root:
            _write(g, topo, core, to, T.o_sb[:, c0:c1], T.o_sb[:, c0:c1], S.ha, S.sent, NE_ON)
            sent += NE_ON
        else:
            i = [j for j, p in enumerate(pl["pieces"]) if p[0] == core][0]
            _, off, a0, a1 = pl["pieces"][i]
            if a1 - a0 != wd:
                g.wait_ge(S.ha, NE_ON)
            _write(g, topo, core, root, T.land[:, off:off + a1 - a0], T.o_sb[:, a0:a1], S["pa_%d" % i], S.sent, NE_P)
            sent += NE_P
        g.wait_ge(S.sent, sent)
        return

    ve.tensor_copy(T.o_sb[:, :], T.o_ps[:, 0:P]).then_inc(S.od, 1)
    g.sync.wait_ge(S.od, 1)
    g.sync.dma_start(T.y[:, :], T.o_sb[:, :]).then_inc(S.st, 16)
    g.sync.wait_ge(S.st, 16)
    g.wait_ge(S.sent, sent)
